import numpy as np
import ml_dtypes


def mxq(x, axis, fmt="e4m3"):
    dtype, down = {"e4m3": (ml_dtypes.float8_e4m3fn, 7), "e5m2": (ml_dtypes.float8_e5m2, 14)}[fmt]
    v = np.moveaxis(np.asarray(x, np.float32).astype(ml_dtypes.bfloat16).astype(np.float64), axis, -1)
    blocks = v.reshape(v.shape[:-1] + (-1, 32))
    amax = np.abs(blocks).max(-1, keepdims=True)
    byte = np.maximum(np.where(amax > 0, np.frexp(amax)[1] - 1 + 127, 0) - down, 1)
    scale = np.exp2(byte - 127.0)
    codes = (blocks / scale).astype(np.float32).astype(dtype).astype(np.float64)
    return np.moveaxis((codes * scale).reshape(v.shape), -1, axis)


WIDE = False


def mx_kscale(k):
    if not WIDE:
        return np.ones(k)
    levels = np.array([10, -10, 5, -5, 0])
    if k % 512:
        return np.exp2(np.random.permutation(np.resize(levels, k // 32))).repeat(32)
    a = np.empty((k // 512, 16))
    for p in range(k // 512):
        a[p, :8] = np.random.permutation(np.resize(levels, 8))
        for g in range(8):
            far = levels[np.abs(levels - a[p, g]) >= 10]
            a[p, g + 8] = far[np.random.randint(len(far))]
    return np.exp2(a.ravel()).repeat(32)


def f64(x):
    return np.asarray(x).astype(np.float64)


def striped(idx):
    return np.tile(idx.reshape(-1, 16).T, (8, 1)).astype(np.uint16)


def unstriped(offs):
    return offs[:16].T.reshape(-1).astype(np.int64)


E2M1 = np.array([0.0, 0.5, 1.0, 1.5, 2.0, 3.0, 4.0, 6.0, -0.0, -0.5, -1.0, -1.5, -2.0, -3.0, -4.0, -6.0])


def pack_weight(w, fmt):
    k, n = w.shape
    w = f64(np.asarray(w, np.float32).astype(ml_dtypes.bfloat16)).reshape(k // 32, 32, n)
    amax = np.abs(w).max(1)
    if fmt == "e4m3":
        byte = np.frexp(amax)[1] - 1 + 127 - 7
    else:
        mant, ex = np.frexp(amax / 6.0)
        byte = np.where(mant > 0.5, ex, ex - 1) + 127
    byte = np.clip(np.where(amax > 0, byte, 1), 1, 254)
    scaled = (w * np.exp2(127.0 - byte)[:, None, :]).reshape(k, n).astype(np.float32)
    by_word = np.ascontiguousarray(scaled.reshape(k // 512, 128, 4, n).transpose(0, 1, 3, 2))
    if fmt == "e4m3":
        words = by_word.astype(ml_dtypes.float8_e4m3fn).view(np.uint8)
    else:
        c = by_word.astype(ml_dtypes.float4_e2m1fn).view(np.uint8) & 0xF
        words = (c[..., 0::2] | (c[..., 1::2] << 4)).reshape(k // 512, 128, 2 * n)
    return np.ascontiguousarray(words), np.ascontiguousarray(byte.astype(np.uint8).reshape(k // 512, 16, n))


def unpack_weight(words, scales, fmt):
    g, _, n = scales.shape
    words = np.ascontiguousarray(words).reshape(g, 128, n, -1)
    if fmt == "e4m3":
        vals = words.view(ml_dtypes.float8_e4m3fn).astype(np.float64)
    else:
        nib = np.empty((g, 128, n, 4), np.uint8)
        nib[..., 0::2] = words & 0xF
        nib[..., 1::2] = words >> 4
        vals = E2M1[nib]
    vals = vals * np.repeat(np.exp2(scales.astype(np.float64) - 127.0), 8, axis=1)[..., None]
    return vals.transpose(0, 1, 3, 2).reshape(g * 512, n)


def gelu(v):
    return 0.5 * v * (1.0 + np.tanh(np.sqrt(2.0 / np.pi) * (v + 0.044715 * v**3)))


K, KA, H, T, S, T2, S2, T3 = 1024, 512, 1024, 2048, 1024, 2048, 512, 2048

def setup_inputs():
    n = np.random.standard_normal
    s = mx_kscale(K)[:, None]
    u = mx_kscale(H)[:, None]
    tab_words, tab_scales = pack_weight(n((K, T)) * s, "e4m3")
    w4_words, w4_scales = pack_weight(1.4 * n((K - KA, H)) / np.sqrt(K) / s[KA:], "e2m1")
    tab2_words, tab2_scales = pack_weight(n((H, T3)) / np.sqrt(H) / u, "e4m3")
    return {
        "tab_words": tab_words, "tab_scales": tab_scales,
        "offs": striped(np.random.permutation(T)[:S]),
        "w1": (1.4 * n((KA, H)) / np.sqrt(K) / s[:KA]).astype(np.float32),
        "w4_words": w4_words, "w4_scales": w4_scales,
        "b1": (0.8 * n(H)).astype(np.float32),
        "gain": (2.5 * np.exp(0.3 * n(H)) * u[:, 0]).astype(np.float32),
        "tab2_words": tab2_words, "tab2_scales": tab2_scales,
        "offs2": striped(np.random.permutation(T3)[:S2]),
        "thr": (0.8 * n(S2)).astype(np.float32),
        "wgo": np.exp(0.3 * n((128, S))).astype(np.float32),
        "page1": (0.6 * n((S2, T2))).astype(np.float32),
        "offs3": striped(np.random.permutation(T2)[:S]),
    }

def reference(tab_words, tab_scales, offs, w1, w4_words, w4_scales, b1, gain,
              tab2_words, tab2_scales, offs2, thr, wgo, page1, offs3):
    v = unpack_weight(tab_words, tab_scales, "e4m3")[:, unstriped(offs)]
    v2 = unpack_weight(tab2_words, tab2_scales, "e4m3")[:, unstriped(offs2)]
    w1q = mxq(f64(w1), 0, "e4m3")
    w4 = unpack_weight(w4_words, w4_scales, "e2m1")
    f = w1q.T @ v[:KA] + w4.T @ v[KA:]
    h = f64(gain)[:, None] * np.tanh(f + f64(b1)[:, None])
    hq = mxq(h, 0, "e4m3")
    e = v2.T @ hq
    score = 1.0 / (1.0 + np.exp(-(e + f64(thr)[:, None])))
    out = f64(page1).copy()
    out[:, unstriped(offs3)] = np.tile(f64(wgo), (S2 // 128, 1)) * score
    return out

@@ -1,0 +1,254 @@
+from contextlib import ExitStack
+
+import concourse.mybir as mybir
+
+K, KA, H, T, S, T2, S2, T3 = 1024, 512, 1024, 2048, 1024, 2048, 512, 2048
+FLOPS = 2 * K * H * S + 2 * H * S2 * S
+
+F32 = mybir.dt.float32
+BF16 = mybir.dt.bfloat16
+I32 = mybir.dt.int32
+U32 = mybir.dt.uint32
+U16 = mybir.dt.uint16
+U8 = mybir.dt.uint8
+FP8X4 = mybir.dt.float8_e4m3fn_x4
+FP4X4 = mybir.dt.float4_e2m1fn_x4
+ACT = mybir.ActivationFunctionType
+MULT = mybir.AluOpType.mult
+
+P = 128
+PACK = 4
+KP = P * PACK
+NB = H // KP
+NC = 512
+CH = S // NC
+MT = S2 // P
+LC = NC // 16
+
+
+def tile_list_slalom_gate_scores_kernel(
+    tc, tab_words, tab_scales, offs, w1, w4_words, w4_scales, b1, gain,
+    tab2_words, tab2_scales, offs2, thr, wgo, page1, offs3, out,
+):
+    nc = tc.nc
+    with ExitStack() as ctx:
+        lists = ctx.enter_context(tc.tile_pool(name="lists", bufs=1))
+        keep = ctx.enter_context(tc.tile_pool(name="keep", bufs=1))
+        mix = ctx.enter_context(tc.tile_pool(name="mix", bufs=1))
+        work = ctx.enter_context(tc.tile_pool(name="work", bufs=2))
+        banks = ctx.enter_context(tc.psum_pool(name="banks", bufs=1))
+
+        def held(name, shape, dtype):
+            return keep.tile(shape, dtype, name=name, align_bytes=64)
+
+        offs_t = lists.tile([P, S // 16], U16, name="offs_t")
+        offs2_t = lists.tile([P, S2 // 16], U16, name="offs2_t")
+        offs3_t = lists.tile([P, S // 16], U16, name="offs3_t")
+
+        tabw = [held("tabw%d" % a, [P, T], U32) for a in range(2)]
+        tab2w = [keep.tile([P, T3], U32, name="tab2w%d" % a, tag="late%d" % a, align_bytes=64) for a in range(2)]
+        tabs = held("tabs", [P, T], U8)
+        tab2s = held("tab2s", [P, T3], U8)
+        w4w = held("w4w", [P, 2 * H], U8)
+        w4s = held("w4s", [P, H], U8)
+        w4wp = held("w4wp", [P, 2 * H], U8)
+        w4sp = held("w4sp", [P, H], U8)
+        w1raw = [keep.tile([P, PACK, KP], F32, name="w1raw%d" % b, tag="raw%d" % b, align_bytes=64) for b in range(NB)]
+        w1q = [held("w1q%d" % b, [P, KP], U32) for b in range(NB)]
+        w1s = [held("w1s%d" % b, [P, KP], U8) for b in range(NB)]
+        b1_t = held("b1_t", [P, NB, PACK], F32)
+        gain_t = held("gain_t", [P, NB, PACK], F32)
+        thr_t = held("thr_t", [P, MT], F32)
+        wgo_t = held("wgo_t", [P, S], F32)
+        page = [held("page%d" % m, [P, T2], F32) for m in range(MT)]
+        vw = [[held("vw%d_%d" % (c, a), [P, NC], U32) for a in range(2)] for c in range(CH)]
+        vs = [held("vs%d" % c, [P, NC], U8) for c in range(CH)]
+        hq = [[held("hq0_%d" % b, [P, NC], U32) for b in range(NB)], []]
+        hs = [[held("hs%d_%d" % (c, b), [P, NC], U8) for b in range(NB)] for c in range(CH)]
+
+        nc.vector.memset(w4s[:].bitcast(I32), 0)
+        nc.vector.memset(tabs[:].bitcast(I32), 0)
+        nc.vector.memset(tab2s[:].bitcast(I32), 0)
+
+        def load_words(dst, src, a):
+            nc.sync.dma_start(out=dst[:].bitcast(I32), in_=src[a].rearrange("p t i -> p (t i)").bitcast(I32))
+
+        def load_w1(b):
+            nc.sync.dma_start(
+                out=w1raw[b][:], in_=w1[:, KP * b : KP * (b + 1)].rearrange("(p j) c -> p j c", j=PACK)
+            )
+
+        def load_tab_scales(a, first, quadrants):
+            for q in quadrants:
+                nc.sync.dma_start(
+                    out=tabs[32 * q + first : 32 * q + first + 4, :].bitcast(I32),
+                    in_=tab_scales[a, 4 * q : 4 * q + 4, :].bitcast(I32),
+                )
+
+        nc.sync.dma_start(offs_t[:], offs)
+        nc.sync.dma_start(out=w4w[:].bitcast(I32), in_=w4_words[0].bitcast(I32))
+        load_words(tabw[1], tab_words, 1)
+        nc.sync.dma_start(out=b1_t[:], in_=b1.rearrange("(b p t) -> p b t", p=P, t=PACK))
+        nc.sync.dma_start(out=gain_t[:], in_=gain.rearrange("(b p t) -> p b t", p=P, t=PACK))
+        nc.sync.dma_start(offs2_t[:], offs2)
+        nc.sync.dma_start(offs3_t[:], offs3)
+        load_words(tabw[0], tab_words, 0)
+        for q in range(4):
+            nc.sync.dma_start(
+                out=w4s[32 * q : 32 * q + 4, :].bitcast(I32), in_=w4_scales[0, 4 * q : 4 * q + 4, :].bitcast(I32)
+            )
+        load_tab_scales(1, 0, range(2))
+        load_w1(0)
+        load_tab_scales(1, 0, range(2, 4))
+        load_tab_scales(0, 4, range(4))
+        load_w1(1)
+        load_words(tab2w[0], tab2_words, 0)
+        for q in range(4):
+            nc.sync.dma_start(
+                out=tab2s[32 * q : 32 * q + 8, :].bitcast(I32), in_=tab2_scales[:, 4 * q : 4 * q + 4, :].bitcast(I32)
+            )
+        with nc.allow_non_contiguous_dma(reason="one threshold a partition"):
+            nc.sync.dma_start(out=thr_t[:], in_=thr.rearrange("(m p) -> p m", p=P))
+        load_words(tab2w[1], tab2_words, 1)
+        nc.sync.dma_start(out=wgo_t[:], in_=wgo)
+        for m in range(MT):
+            nc.sync.dma_start(out=page[m][:], in_=page1[P * m : P * (m + 1), :])
+
+        nc.vector.tensor_copy(
+            out=w4wp[:].bitcast(U16).rearrange("p (b t q) -> p b q t", b=NB, t=PACK),
+            in_=w4w[:].bitcast(U16).rearrange("p (b q t) -> p b q t", b=NB, t=PACK),
+        )
+
+        def gather(dst, window, offsets):
+            nc.vector.tensor_copy(dst[:], window[:].indirect(offsets))
+
+        def chunk_offs(lst, c):
+            return lst[:, LC * c : LC * (c + 1)]
+
+        def round_w1(b):
+            wb = mix.tile([P, KP * PACK], BF16, name="wb%d" % b, align_bytes=64, offset=2 * KP * PACK * b)
+            nc.scalar.copy(
+                out=wb[:].rearrange("p (t u v j) -> p u j v t", t=PACK, v=2, j=PACK),
+                in_=w1raw[b][:].rearrange("p j (u v t) -> p u j v t", v=2, t=PACK),
+            )
+            return wb
+
+        def quantize(codes, scales, src, lo=0, hi=NC):
+            nc.vector.quantize_mx(
+                out=codes[:, lo:hi].bitcast(FP8X4), scales=scales[:, lo:hi], in_=src[:, PACK * lo : PACK * hi]
+            )
+
+        def bank_tile(bank, width):
+            return banks.tile([P, width], F32, name="acc", tag="bank%d" % bank)
+
+        def features(c, b, bank_of):
+            th = keep.tile([P, PACK, NC], F32, name="th%d_%d" % (c, b), tag="raw%d" % (2 * c + 1 - b), align_bytes=64)
+            for t in range(PACK):
+                g = PACK * b + t
+                acc = bank_tile(bank_of[t], NC)
+                exit_pass = dict(
+                    lhsT=w4wp[:, 2 * P * g : 2 * P * (g + 1)].bitcast(FP4X4),
+                    lhsT_scale=w4sp[:, P * g : P * (g + 1)],
+                    rhs=vw[c][1][:].bitcast(FP8X4),
+                    rhs_scale=vs[c][:],
+                )
+                approach_pass = dict(
+                    lhsT=w1q[b][:, P * t : P * (t + 1)].bitcast(FP8X4),
+                    lhsT_scale=w1s[b][:, P * t : P * (t + 1)],
+                    rhs=vw[c][0][:].bitcast(FP8X4),
+                    rhs_scale=vs[c][4:P, :],
+                )
+                passes = (exit_pass, approach_pass) if b == 0 else (approach_pass, exit_pass)
+                nc.tensor.matmul_mx(out=acc[:], start=True, stop=False, **passes[0])
+                nc.tensor.matmul_mx(out=acc[:], start=False, stop=True, **passes[1])
+                nc.scalar.activation(out=th[:, t, :], in_=acc[:], func=ACT.Tanh, bias=b1_t[:, b, t : t + 1])
+            return th
+
+        def gain_on_vector(b, th, hb, lo, hi):
+            nc.vector.tensor_tensor(
+                out=hb[:, PACK * lo : PACK * hi].rearrange("p (u i t) -> p u t i", i=4, t=PACK),
+                in0=th[:, :, lo:hi].rearrange("p t (u i) -> p u t i", i=4),
+                in1=gain_t[:, b, :].unsqueeze(1).unsqueeze(3).to_broadcast([P, (hi - lo) // 4, PACK, 4]),
+                op=MULT,
+            )
+
+        def gain_on_scalar(b, th):
+            planes = keep.tile([P, PACK, NC], BF16, name="planes%d" % b, tag="late%d" % (2 - b), align_bytes=64)
+            for t in range(PACK):
+                nc.scalar.activation(out=planes[:, t, :], in_=th[:, t, :], func=ACT.Copy, scale=gain_t[:, b, t : t + 1])
+            return planes
+
+        def weave_on_scalar(planes):
+            hb = work.tile([P, NC * PACK], BF16, name="hb", align_bytes=64)
+            nc.scalar.copy(
+                out=hb[:].rearrange("p (u i t) -> p u t i", i=8, t=PACK),
+                in_=planes[:].rearrange("p t (u i) -> p u t i", i=8),
+            )
+            return hb
+
+        def scores(c, m, bank, lo=0, hi=NC, slot=None):
+            acc = bank_tile(bank, hi - lo)
+            for a in range(NB):
+                nc.tensor.matmul_mx(
+                    out=acc[:],
+                    lhsT=v2w[a][:, P * m : P * (m + 1)].bitcast(FP8X4),
+                    lhsT_scale=v2s[4 * a : P, P * m : P * (m + 1)],
+                    rhs=hq[c][a][:, lo:hi].bitcast(FP8X4),
+                    rhs_scale=hs[c][a][:, lo:hi],
+                    start=(a == 0),
+                    stop=(a == NB - 1),
+                )
+            if slot is None:
+                sc = work.tile([P, hi - lo], F32, name="sc", bufs=6)
+            else:
+                sc = keep.tile([P, hi - lo], F32, name="sc_held", tag=slot, align_bytes=64)
+            nc.scalar.activation(out=sc[:], in_=acc[:], func=ACT.Sigmoid, bias=thr_t[:, m : m + 1])
+            first, last = NC * c + lo, NC * c + hi
+            nc.vector.tensor_tensor(
+                page[m][:].indirect(offs3_t[:, first // 16 : last // 16]), sc[:], wgo_t[:, first:last], MULT
+            )
+
+        for c in range(CH):
+            gather(vw[c][1], tabw[1], chunk_offs(offs_t, c))
+        gather(vs[0], tabs, chunk_offs(offs_t, 0))
+        nc.vector.tensor_copy(
+            out=w4sp[:].rearrange("p (b t q) -> p b q t", b=NB, t=PACK),
+            in_=w4s[:].rearrange("p (b q t) -> p b q t", b=NB, t=PACK),
+        )
+        for c in range(CH):
+            gather(vw[c][0], tabw[0], chunk_offs(offs_t, c))
+        wb0 = round_w1(0)
+        wb1 = round_w1(1)
+        quantize(w1q[0], w1s[0], wb0)
+        gather(vs[1], tabs, chunk_offs(offs_t, 1))
+        quantize(w1q[1], w1s[1], wb1)
+        v2w = [
+            mix.tile([P, S2], U32, name="v2w0", align_bytes=64, offset=0),
+            mix.tile([P, S2], U32, name="v2w1", align_bytes=64, offset=2 * KP * PACK),
+        ]
+        v2s = mix.tile([P, S2], U8, name="v2s", align_bytes=64, offset=2 * KP * PACK + 4 * S2)
+        gather(v2w[0], tab2w[0], offs2_t[:])
+        gather(v2s, tab2s, offs2_t[:])
+        gather(v2w[1], tab2w[1], offs2_t[:])
+        th00 = features(0, 0, (0, 1, 2, 3))
+        th01 = features(0, 1, (4, 5, 6, 7))
+        hb00 = keep.tile([P, NC * PACK], BF16, name="hb00", tag="late1", align_bytes=64)
+        gain_on_vector(0, th00, hb00, 0, NC)
+        quantize(hq[0][0], hs[0][0], hb00)
+        hb01 = keep.tile([P, NC * PACK], BF16, name="hb01", tag="raw1", align_bytes=64)
+        half = NC // 2
+        for lo in (0, half):
+            gain_on_vector(1, th01, hb01, lo, lo + half)
+            quantize(hq[0][1], hs[0][1], hb01, lo, lo + half)
+        scores(0, 0, 0, 0, half)
+        scores(0, 0, 1, half, NC)
+        scores(0, 1, 2, slot="turn0")
+        scores(0, 2, 3, slot="turn1")
+        for b, bank_of in enumerate(((4, 5, 6, 0), (1, 2, 3, 0))):
+            hb = weave_on_scalar(gain_on_scalar(b, features(1, b, bank_of)))
+            hq[1].append(keep.tile([P, NC], U32, name="hq1_%d" % b, tag="turn%d" % b, align_bytes=64))
+            quantize(hq[1][b], hs[1][b], hb)
+        scores(0, 3, 7, slot="late1")
+        for m, bank in enumerate((4, 5, 6, 7)):
+            scores(1, m, bank)
+            nc.sync.dma_start(out=out[P * m : P * (m + 1), :], in_=page[m][:])

@@ -48,7 +48,7 @@ def tile_list_slalom_gate_scores_kernel(
         tabw = [held("tabw%d" % a, [P, T], U32) for a in range(2)]
         tab2w = [keep.tile([P, T3], U32, name="tab2w%d" % a, tag="late%d" % a, align_bytes=64) for a in range(2)]
         tabs = held("tabs", [P, T], U8)
-        tab2s = held("tab2s", [P, T3], U8)
+        tab2s = keep.tile([P, T3], U8, name="tab2s", tag="late3", align_bytes=64)
         w4w = held("w4w", [P, 2 * H], U8)
         w4s = held("w4s", [P, H], U8)
         w4wp = held("w4wp", [P, 2 * H], U8)
@@ -66,7 +66,7 @@ def tile_list_slalom_gate_scores_kernel(
         hq = [[held("hq0_%d" % b, [P, NC], U32) for b in range(NB)], []]
         hs = [[held("hs%d_%d" % (c, b), [P, NC], U8) for b in range(NB)] for c in range(CH)]
 
-        nc.vector.memset(w4s[:].bitcast(I32), 0)
+        nc.gpsimd.memset(w4s[:].bitcast(I32), 0)
         nc.vector.memset(tabs[:].bitcast(I32), 0)
         nc.vector.memset(tab2s[:].bitcast(I32), 0)
 
@@ -78,38 +78,41 @@ def tile_list_slalom_gate_scores_kernel(
                 out=w1raw[b][:], in_=w1[:, KP * b : KP * (b + 1)].rearrange("(p j) c -> p j c", j=PACK)
             )
 
-        def load_tab_scales(a, first, quadrants):
-            for q in quadrants:
-                nc.sync.dma_start(
-                    out=tabs[32 * q + first : 32 * q + first + 4, :].bitcast(I32),
-                    in_=tab_scales[a, 4 * q : 4 * q + 4, :].bitcast(I32),
-                )
+        def load_tab_scales(rows):
+            for r in rows:
+                for a, first in ((1, 0), (0, 4)):
+                    nc.sync.dma_start(
+                        out=tabs[first + r : P : 32, :].bitcast(I32), in_=tab_scales[a, r:16:4, :].bitcast(I32)
+                    )
+
+        for r in range(4):
+            nc.gpsimd.dma_start(out=w4s[r:P:32, :].bitcast(I32), in_=w4_scales[0, r:16:4, :].bitcast(I32))
 
         nc.sync.dma_start(offs_t[:], offs)
-        nc.sync.dma_start(out=w4w[:].bitcast(I32), in_=w4_words[0].bitcast(I32))
-        load_words(tabw[1], tab_words, 1)
-        nc.sync.dma_start(out=b1_t[:], in_=b1.rearrange("(b p t) -> p b t", p=P, t=PACK))
-        nc.sync.dma_start(out=gain_t[:], in_=gain.rearrange("(b p t) -> p b t", p=P, t=PACK))
+        for b in range(NB):
+            cols = slice(2 * KP * b, 2 * KP * (b + 1))
+            nc.sync.dma_start(out=w4w[:, cols].bitcast(I32), in_=w4_words[0, :, cols].bitcast(I32))
+        for cols in (slice(0, T // 2), slice(T // 2, T)):
+            nc.sync.dma_start(
+                out=tabw[1][:, cols].bitcast(I32), in_=tab_words[1, :, cols, :].rearrange("p t i -> p (t i)").bitcast(I32)
+            )
         nc.sync.dma_start(offs2_t[:], offs2)
         nc.sync.dma_start(offs3_t[:], offs3)
         load_words(tabw[0], tab_words, 0)
-        for q in range(4):
-            nc.sync.dma_start(
-                out=w4s[32 * q : 32 * q + 4, :].bitcast(I32), in_=w4_scales[0, 4 * q : 4 * q + 4, :].bitcast(I32)
-            )
-        load_tab_scales(1, 0, range(2))
+        load_tab_scales(range(3))
         load_w1(0)
-        load_tab_scales(1, 0, range(2, 4))
-        load_tab_scales(0, 4, range(4))
+        load_tab_scales(range(3, 4))
         load_w1(1)
+        nc.sync.dma_start(out=b1_t[:], in_=b1.rearrange("(b p t) -> p b t", p=P, t=PACK))
         load_words(tab2w[0], tab2_words, 0)
+        nc.sync.dma_start(out=gain_t[:], in_=gain.rearrange("(b p t) -> p b t", p=P, t=PACK))
+        load_words(tab2w[1], tab2_words, 1)
         for q in range(4):
             nc.sync.dma_start(
                 out=tab2s[32 * q : 32 * q + 8, :].bitcast(I32), in_=tab2_scales[:, 4 * q : 4 * q + 4, :].bitcast(I32)
             )
         with nc.allow_non_contiguous_dma(reason="one threshold a partition"):
             nc.sync.dma_start(out=thr_t[:], in_=thr.rearrange("(m p) -> p m", p=P))
-        load_words(tab2w[1], tab2_words, 1)
         nc.sync.dma_start(out=wgo_t[:], in_=wgo)
         for m in range(MT):
             nc.sync.dma_start(out=page[m][:], in_=page1[P * m : P * (m + 1), :])
@@ -166,9 +169,9 @@ def tile_list_slalom_gate_scores_kernel(
 
         def gain_on_vector(b, th, hb, lo, hi):
             nc.vector.tensor_tensor(
-                out=hb[:, PACK * lo : PACK * hi].rearrange("p (u i t) -> p u t i", i=4, t=PACK),
-                in0=th[:, :, lo:hi].rearrange("p t (u i) -> p u t i", i=4),
-                in1=gain_t[:, b, :].unsqueeze(1).unsqueeze(3).to_broadcast([P, (hi - lo) // 4, PACK, 4]),
+                out=hb[:, PACK * lo : PACK * hi].rearrange("p (u i t) -> p u t i", i=2, t=PACK),
+                in0=th[:, :, lo:hi].rearrange("p t (u i) -> p u t i", i=2),
+                in1=gain_t[:, b, :].unsqueeze(1).unsqueeze(3).to_broadcast([P, (hi - lo) // 2, PACK, 2]),
                 op=MULT,
             )
 
@@ -181,8 +184,8 @@ def tile_list_slalom_gate_scores_kernel(
         def weave_on_scalar(planes):
             hb = work.tile([P, NC * PACK], BF16, name="hb", align_bytes=64)
             nc.scalar.copy(
-                out=hb[:].rearrange("p (u i t) -> p u t i", i=8, t=PACK),
-                in_=planes[:].rearrange("p t (u i) -> p u t i", i=8),
+                out=hb[:].rearrange("p (u i t) -> p u t i", i=4, t=PACK),
+                in_=planes[:].rearrange("p t (u i) -> p u t i", i=4),
             )
             return hb
 
@@ -228,11 +231,11 @@ def tile_list_slalom_gate_scores_kernel(
         ]
         v2s = mix.tile([P, S2], U8, name="v2s", align_bytes=64, offset=2 * KP * PACK + 4 * S2)
         gather(v2w[0], tab2w[0], offs2_t[:])
-        gather(v2s, tab2s, offs2_t[:])
         gather(v2w[1], tab2w[1], offs2_t[:])
+        gather(v2s, tab2s, offs2_t[:])
         th00 = features(0, 0, (0, 1, 2, 3))
         th01 = features(0, 1, (4, 5, 6, 7))
-        hb00 = keep.tile([P, NC * PACK], BF16, name="hb00", tag="late1", align_bytes=64)
+        hb00 = keep.tile([P, NC * PACK], BF16, name="hb00", tag="late3", align_bytes=64)
         gain_on_vector(0, th00, hb00, 0, NC)
         quantize(hq[0][0], hs[0][0], hb00)
         hb01 = keep.tile([P, NC * PACK], BF16, name="hb01", tag="raw1", align_bytes=64)

from contextlib import ExitStack

import concourse.mybir as mybir

K, KA, H, T, S, T2, S2, T3 = 1024, 512, 1024, 2048, 1024, 2048, 512, 2048
FLOPS = 2 * K * H * S + 2 * H * S2 * S

F32 = mybir.dt.float32
BF16 = mybir.dt.bfloat16
I32 = mybir.dt.int32
U32 = mybir.dt.uint32
U16 = mybir.dt.uint16
U8 = mybir.dt.uint8
FP8X4 = mybir.dt.float8_e4m3fn_x4
FP4X4 = mybir.dt.float4_e2m1fn_x4
ACT = mybir.ActivationFunctionType
MULT = mybir.AluOpType.mult

P = 128
PACK = 4
KP = P * PACK
NB = H // KP
NC = 512
CH = S // NC
MT = S2 // P
LC = NC // 16


def tile_list_slalom_gate_scores_kernel(
    tc, tab_words, tab_scales, offs, w1, w4_words, w4_scales, b1, gain,
    tab2_words, tab2_scales, offs2, thr, wgo, page1, offs3, out,
):
    nc = tc.nc
    with ExitStack() as ctx:
        lists = ctx.enter_context(tc.tile_pool(name="lists", bufs=1))
        keep = ctx.enter_context(tc.tile_pool(name="keep", bufs=1))
        mix = ctx.enter_context(tc.tile_pool(name="mix", bufs=1))
        work = ctx.enter_context(tc.tile_pool(name="work", bufs=2))
        banks = ctx.enter_context(tc.psum_pool(name="banks", bufs=1))

        def held(name, shape, dtype):
            return keep.tile(shape, dtype, name=name, align_bytes=64)

        offs_t = lists.tile([P, S // 16], U16, name="offs_t")
        offs2_t = lists.tile([P, S2 // 16], U16, name="offs2_t")
        offs3_t = lists.tile([P, S // 16], U16, name="offs3_t")

        tabw = [held("tabw%d" % a, [P, T], U32) for a in range(2)]
        tab2w = [keep.tile([P, T3], U32, name="tab2w%d" % a, tag="late%d" % a, align_bytes=64) for a in range(2)]
        tabs = held("tabs", [P, T], U8)
        tab2s = keep.tile([P, T3], U8, name="tab2s", tag="late3", align_bytes=64)
        w4w = held("w4w", [P, 2 * H], U8)
        w4s = held("w4s", [P, H], U8)
        w4wp = held("w4wp", [P, 2 * H], U8)
        w4sp = held("w4sp", [P, H], U8)
        w1raw = [keep.tile([P, PACK, KP], F32, name="w1raw%d" % b, tag="raw%d" % b, align_bytes=64) for b in range(NB)]
        w1q = [held("w1q%d" % b, [P, KP], U32) for b in range(NB)]
        w1s = [held("w1s%d" % b, [P, KP], U8) for b in range(NB)]
        b1_t = held("b1_t", [P, NB, PACK], F32)
        gain_t = held("gain_t", [P, NB, PACK], F32)
        thr_t = held("thr_t", [P, MT], F32)
        wgo_t = held("wgo_t", [P, S], F32)
        page = [held("page%d" % m, [P, T2], F32) for m in range(MT)]
        vw = [[held("vw%d_%d" % (c, a), [P, NC], U32) for a in range(2)] for c in range(CH)]
        vs = [held("vs%d" % c, [P, NC], U8) for c in range(CH)]
        hq = [[held("hq0_%d" % b, [P, NC], U32) for b in range(NB)], []]
        hs = [[held("hs%d_%d" % (c, b), [P, NC], U8) for b in range(NB)] for c in range(CH)]

        nc.gpsimd.memset(w4s[:].bitcast(I32), 0)
        nc.vector.memset(tabs[:].bitcast(I32), 0)
        nc.vector.memset(tab2s[:].bitcast(I32), 0)

        def load_words(dst, src, a):
            nc.sync.dma_start(out=dst[:].bitcast(I32), in_=src[a].rearrange("p t i -> p (t i)").bitcast(I32))

        def load_w1(b):
            nc.sync.dma_start(
                out=w1raw[b][:], in_=w1[:, KP * b : KP * (b + 1)].rearrange("(p j) c -> p j c", j=PACK)
            )

        def load_tab_scales(rows):
            for r in rows:
                for a, first in ((1, 0), (0, 4)):
                    nc.sync.dma_start(
                        out=tabs[first + r : P : 32, :].bitcast(I32), in_=tab_scales[a, r:16:4, :].bitcast(I32)
                    )

        for r in range(4):
            nc.gpsimd.dma_start(out=w4s[r:P:32, :].bitcast(I32), in_=w4_scales[0, r:16:4, :].bitcast(I32))

        nc.sync.dma_start(offs_t[:], offs)
        for b in range(NB):
            cols = slice(2 * KP * b, 2 * KP * (b + 1))
            nc.sync.dma_start(out=w4w[:, cols].bitcast(I32), in_=w4_words[0, :, cols].bitcast(I32))
        for cols in (slice(0, T // 2), slice(T // 2, T)):
            nc.sync.dma_start(
                out=tabw[1][:, cols].bitcast(I32), in_=tab_words[1, :, cols, :].rearrange("p t i -> p (t i)").bitcast(I32)
            )
        nc.sync.dma_start(offs2_t[:], offs2)
        nc.sync.dma_start(offs3_t[:], offs3)
        load_words(tabw[0], tab_words, 0)
        load_tab_scales(range(3))
        load_w1(0)
        load_tab_scales(range(3, 4))
        load_w1(1)
        nc.sync.dma_start(out=b1_t[:], in_=b1.rearrange("(b p t) -> p b t", p=P, t=PACK))
        load_words(tab2w[0], tab2_words, 0)
        nc.sync.dma_start(out=gain_t[:], in_=gain.rearrange("(b p t) -> p b t", p=P, t=PACK))
        load_words(tab2w[1], tab2_words, 1)
        for q in range(4):
            nc.sync.dma_start(
                out=tab2s[32 * q : 32 * q + 8, :].bitcast(I32), in_=tab2_scales[:, 4 * q : 4 * q + 4, :].bitcast(I32)
            )
        with nc.allow_non_contiguous_dma(reason="one threshold a partition"):
            nc.sync.dma_start(out=thr_t[:], in_=thr.rearrange("(m p) -> p m", p=P))
        nc.sync.dma_start(out=wgo_t[:], in_=wgo)
        for m in range(MT):
            nc.sync.dma_start(out=page[m][:], in_=page1[P * m : P * (m + 1), :])

        nc.vector.tensor_copy(
            out=w4wp[:].bitcast(U16).rearrange("p (b t q) -> p b q t", b=NB, t=PACK),
            in_=w4w[:].bitcast(U16).rearrange("p (b q t) -> p b q t", b=NB, t=PACK),
        )

        def gather(dst, window, offsets):
            nc.vector.tensor_copy(dst[:], window[:].indirect(offsets))

        def chunk_offs(lst, c):
            return lst[:, LC * c : LC * (c + 1)]

        def round_w1(b):
            wb = mix.tile([P, KP * PACK], BF16, name="wb%d" % b, align_bytes=64, offset=2 * KP * PACK * b)
            nc.scalar.copy(
                out=wb[:].rearrange("p (t u v j) -> p u j v t", t=PACK, v=2, j=PACK),
                in_=w1raw[b][:].rearrange("p j (u v t) -> p u j v t", v=2, t=PACK),
            )
            return wb

        def quantize(codes, scales, src, lo=0, hi=NC):
            nc.vector.quantize_mx(
                out=codes[:, lo:hi].bitcast(FP8X4), scales=scales[:, lo:hi], in_=src[:, PACK * lo : PACK * hi]
            )

        def bank_tile(bank, width):
            return banks.tile([P, width], F32, name="acc", tag="bank%d" % bank)

        def features(c, b, bank_of):
            th = keep.tile([P, PACK, NC], F32, name="th%d_%d" % (c, b), tag="raw%d" % (2 * c + 1 - b), align_bytes=64)
            for t in range(PACK):
                g = PACK * b + t
                acc = bank_tile(bank_of[t], NC)
                exit_pass = dict(
                    lhsT=w4wp[:, 2 * P * g : 2 * P * (g + 1)].bitcast(FP4X4),
                    lhsT_scale=w4sp[:, P * g : P * (g + 1)],
                    rhs=vw[c][1][:].bitcast(FP8X4),
                    rhs_scale=vs[c][:],
                )
                approach_pass = dict(
                    lhsT=w1q[b][:, P * t : P * (t + 1)].bitcast(FP8X4),
                    lhsT_scale=w1s[b][:, P * t : P * (t + 1)],
                    rhs=vw[c][0][:].bitcast(FP8X4),
                    rhs_scale=vs[c][4:P, :],
                )
                passes = (exit_pass, approach_pass) if b == 0 else (approach_pass, exit_pass)
                nc.tensor.matmul_mx(out=acc[:], start=True, stop=False, **passes[0])
                nc.tensor.matmul_mx(out=acc[:], start=False, stop=True, **passes[1])
                nc.scalar.activation(out=th[:, t, :], in_=acc[:], func=ACT.Tanh, bias=b1_t[:, b, t : t + 1])
            return th

        def gain_on_vector(b, th, hb, lo, hi):
            nc.vector.tensor_tensor(
                out=hb[:, PACK * lo : PACK * hi].rearrange("p (u i t) -> p u t i", i=2, t=PACK),
                in0=th[:, :, lo:hi].rearrange("p t (u i) -> p u t i", i=2),
                in1=gain_t[:, b, :].unsqueeze(1).unsqueeze(3).to_broadcast([P, (hi - lo) // 2, PACK, 2]),
                op=MULT,
            )

        def gain_on_scalar(b, th):
            planes = keep.tile([P, PACK, NC], BF16, name="planes%d" % b, tag="late%d" % (2 - b), align_bytes=64)
            for t in range(PACK):
                nc.scalar.activation(out=planes[:, t, :], in_=th[:, t, :], func=ACT.Copy, scale=gain_t[:, b, t : t + 1])
            return planes

        def weave_on_scalar(planes):
            hb = work.tile([P, NC * PACK], BF16, name="hb", align_bytes=64)
            nc.scalar.copy(
                out=hb[:].rearrange("p (u i t) -> p u t i", i=4, t=PACK),
                in_=planes[:].rearrange("p t (u i) -> p u t i", i=4),
            )
            return hb

        def scores(c, m, bank, lo=0, hi=NC, slot=None):
            acc = bank_tile(bank, hi - lo)
            for a in range(NB):
                nc.tensor.matmul_mx(
                    out=acc[:],
                    lhsT=v2w[a][:, P * m : P * (m + 1)].bitcast(FP8X4),
                    lhsT_scale=v2s[4 * a : P, P * m : P * (m + 1)],
                    rhs=hq[c][a][:, lo:hi].bitcast(FP8X4),
                    rhs_scale=hs[c][a][:, lo:hi],
                    start=(a == 0),
                    stop=(a == NB - 1),
                )
            if slot is None:
                sc = work.tile([P, hi - lo], F32, name="sc", bufs=6)
            else:
                sc = keep.tile([P, hi - lo], F32, name="sc_held", tag=slot, align_bytes=64)
            nc.scalar.activation(out=sc[:], in_=acc[:], func=ACT.Sigmoid, bias=thr_t[:, m : m + 1])
            first, last = NC * c + lo, NC * c + hi
            nc.vector.tensor_tensor(
                page[m][:].indirect(offs3_t[:, first // 16 : last // 16]), sc[:], wgo_t[:, first:last], MULT
            )

        for c in range(CH):
            gather(vw[c][1], tabw[1], chunk_offs(offs_t, c))
        gather(vs[0], tabs, chunk_offs(offs_t, 0))
        nc.vector.tensor_copy(
            out=w4sp[:].rearrange("p (b t q) -> p b q t", b=NB, t=PACK),
            in_=w4s[:].rearrange("p (b q t) -> p b q t", b=NB, t=PACK),
        )
        for c in range(CH):
            gather(vw[c][0], tabw[0], chunk_offs(offs_t, c))
        wb0 = round_w1(0)
        wb1 = round_w1(1)
        quantize(w1q[0], w1s[0], wb0)
        gather(vs[1], tabs, chunk_offs(offs_t, 1))
        quantize(w1q[1], w1s[1], wb1)
        v2w = [
            mix.tile([P, S2], U32, name="v2w0", align_bytes=64, offset=0),
            mix.tile([P, S2], U32, name="v2w1", align_bytes=64, offset=2 * KP * PACK),
        ]
        v2s = mix.tile([P, S2], U8, name="v2s", align_bytes=64, offset=2 * KP * PACK + 4 * S2)
        gather(v2w[0], tab2w[0], offs2_t[:])
        gather(v2w[1], tab2w[1], offs2_t[:])
        gather(v2s, tab2s, offs2_t[:])
        th00 = features(0, 0, (0, 1, 2, 3))
        th01 = features(0, 1, (4, 5, 6, 7))
        hb00 = keep.tile([P, NC * PACK], BF16, name="hb00", tag="late3", align_bytes=64)
        gain_on_vector(0, th00, hb00, 0, NC)
        quantize(hq[0][0], hs[0][0], hb00)
        hb01 = keep.tile([P, NC * PACK], BF16, name="hb01", tag="raw1", align_bytes=64)
        half = NC // 2
        for lo in (0, half):
            gain_on_vector(1, th01, hb01, lo, lo + half)
            quantize(hq[0][1], hs[0][1], hb01, lo, lo + half)
        scores(0, 0, 0, 0, half)
        scores(0, 0, 1, half, NC)
        scores(0, 1, 2, slot="turn0")
        scores(0, 2, 3, slot="turn1")
        for b, bank_of in enumerate(((4, 5, 6, 0), (1, 2, 3, 0))):
            hb = weave_on_scalar(gain_on_scalar(b, features(1, b, bank_of)))
            hq[1].append(keep.tile([P, NC], U32, name="hq1_%d" % b, tag="turn%d" % b, align_bytes=64))
            quantize(hq[1][b], hs[1][b], hb)
        scores(0, 3, 7, slot="late1")
        for m, bank in enumerate((4, 5, 6, 7)):
            scores(1, m, bank)
            nc.sync.dma_start(out=out[P * m : P * (m + 1), :], in_=page[m][:])
